import numpy as np
import ml_dtypes


def mxq(x, axis, fmt="e4m3"):
    dtype, down = {"e4m3": (ml_dtypes.float8_e4m3fn, 7), "e5m2": (ml_dtypes.float8_e5m2, 14)}[fmt]
    v = np.moveaxis(np.asarray(x, np.float32).astype(ml_dtypes.bfloat16).astype(np.float64), axis, -1)
    blocks = v.reshape(v.shape[:-1] + (-1, 32))
    amax = np.abs(blocks).max(-1, keepdims=True)
    byte = np.maximum(np.where(amax > 0, np.frexp(amax)[1] - 1 + 127, 0) - down, 1)
    scale = np.exp2(byte - 127.0)
    codes = (blocks / scale).astype(np.float32).astype(dtype).astype(np.float64)
    return np.moveaxis((codes * scale).reshape(v.shape), -1, axis)


WIDE = False


def mx_kscale(k):
    if not WIDE:
        return np.ones(k)
    levels = np.array([10, -10, 5, -5, 0])
    if k % 512:
        return np.exp2(np.random.permutation(np.resize(levels, k // 32))).repeat(32)
    a = np.empty((k // 512, 16))
    for p in range(k // 512):
        a[p, :8] = np.random.permutation(np.resize(levels, 8))
        for g in range(8):
            far = levels[np.abs(levels - a[p, g]) >= 10]
            a[p, g + 8] = far[np.random.randint(len(far))]
    return np.exp2(a.ravel()).repeat(32)


def f64(x):
    return np.asarray(x).astype(np.float64)


def striped(idx):
    return np.tile(idx.reshape(-1, 16).T, (8, 1)).astype(np.uint16)


def unstriped(offs):
    return offs[:16].T.reshape(-1).astype(np.int64)


def pack_weight(w):
    k, n = w.shape
    w = f64(np.asarray(w, np.float32).astype(ml_dtypes.bfloat16)).reshape(k // 32, 32, n)
    amax = np.abs(w).max(1)
    byte = np.clip(np.where(amax > 0, np.frexp(amax)[1] - 1 + 127 - 7, 1), 1, 254)
    scaled = (w * np.exp2(127.0 - byte)[:, None, :]).reshape(k, n).astype(np.float32)
    words = np.ascontiguousarray(scaled.reshape(k // 512, 128, 4, n).transpose(0, 1, 3, 2)).astype(ml_dtypes.float8_e4m3fn).view(np.uint8)
    return words, np.ascontiguousarray(byte.astype(np.uint8).reshape(k // 512, 16, n))


def unpack_weight(words, scales):
    g, p, n, _ = words.shape
    vals = np.ascontiguousarray(words).view(ml_dtypes.float8_e4m3fn).astype(np.float64) * np.repeat(np.exp2(scales.astype(np.float64) - 127.0), 8, axis=1)[..., None]
    return vals.transpose(0, 1, 3, 2).reshape(g * 512, n)


K, T, S, D, N, V = 1024, 2048, 512, 2, 128, 256
P = 2 ** 7


def setup_inputs():
    n = np.random.standard_normal
    s = mx_kscale(K)[:, None]
    packed_xT = pack_weight(n((K, T)) * s)
    return {
        "x_words": packed_xT[0],
        "x_scales": packed_xT[1],
        "w1": (n((K, N)) / np.sqrt(K) / s).astype(np.float32),
        "w2": (n((K, N)) / np.sqrt(K) / s).astype(np.float32),
        "emb": (np.tile(-np.random.uniform(0.5, 1.5, V), (P, 1))).astype(np.float32),
        "offs": striped(np.random.permutation(T)[:S]),
        "nbr": striped(np.random.permutation(np.concatenate([np.arange(V), np.random.randint(0, V, S - V)]))),
    }


def reference(x_words, x_scales, w1, w2, emb, offs, nbr):
    xq = unpack_weight(x_words, x_scales)[:, unstriped(offs)]
    y = mxq(f64(w1), 0, "e4m3").T @ xq
    rho = np.exp(0.5 * y)
    dens = rho.reshape(len(rho), -1, D).sum(axis=2) + 0.5
    fp = f64(emb)[:1] / np.sqrt(dens)
    z = mxq(f64(w2), 0, "e4m3").T @ xq
    return 0.5 * ((np.repeat(fp, D, axis=1) + fp[:, unstriped(nbr)]) * rho) + z

@@ -1,0 +1,152 @@
+from contextlib import ExitStack
+
+import concourse.mybir as mybir
+
+K, T, S, N, V = 1024, 2048, 512, 128, 256
+FLOPS = 2 * 2 * K * N * S
+
+F32 = mybir.dt.float32
+BF16 = mybir.dt.bfloat16
+I32 = mybir.dt.int32
+U32 = mybir.dt.uint32
+U16 = mybir.dt.uint16
+U8 = mybir.dt.uint8
+FP8X4 = mybir.dt.float8_e4m3fn_x4
+ACT = mybir.ActivationFunctionType
+ALU = mybir.AluOpType
+
+P = 128
+PACK = 4
+PASSES = K // (P * PACK)
+HALF = S // 2
+SPARE = 32
+
+
+def tile_picked_yeamf_force_p_kernel(
+    tc, x_words, x_scales, w1, w2, emb, offs, nbr, out
+):
+    nc = tc.nc
+    with ExitStack() as ctx:
+        sb = ctx.enter_context(tc.tile_pool(name="sb", bufs=1))
+        psum = ctx.enter_context(tc.psum_pool(name="psum", bufs=1))
+
+        offs_sb = sb.tile([P, S // 16], U16, name="offs_sb")
+        nbr_sb = sb.tile([P, S // 16], U16, name="nbr_sb")
+        table_words = [sb.tile([P, T], U32, name=f"table_words{o}", tag=f"table{o}", align_bytes=64) for o in range(PASSES)]
+        table_scales = sb.tile([P, T], U8, name="table_scales", align_bytes=64)
+        w_raw = [sb.tile([P, PASSES, PACK, N], F32, name=f"w_raw{i}", align_bytes=64) for i in range(2)]
+        emb_sb = sb.tile([P, V], F32, name="emb_sb", align_bytes=64)
+        slope = sb.tile([P, V + SPARE], F32, name="slope", align_bytes=64)
+
+        nc.vector.memset(table_scales[:].bitcast(I32), 0)
+        nc.vector.memset(slope[:, V:], 0.0)
+
+        def load_words(o):
+            nc.sync.dma_start(
+                out=table_words[o][:].bitcast(I32),
+                in_=x_words[o].rearrange("p c r -> p (c r)").bitcast(I32),
+            )
+
+        def load_weight(i, w):
+            nc.sync.dma_start(
+                out=w_raw[i][:].rearrange("p g j n -> p g (j n)"),
+                in_=w.rearrange("(g p j) n -> p g (j n)", p=P, j=PACK),
+            )
+
+        nc.sync.dma_start(offs_sb[:], offs)
+        nc.sync.dma_start(nbr_sb[:], nbr)
+        load_words(0)
+        load_weight(0, w1)
+        for q in range(4):
+            nc.sync.dma_start(
+                out=table_scales[32 * q : 32 * q + 4 * PASSES, :].bitcast(I32),
+                in_=x_scales[:, 4 * q : 4 * q + 4, :].bitcast(I32),
+            )
+        load_words(1)
+        load_weight(1, w2)
+        nc.sync.dma_start(out=emb_sb[:], in_=emb)
+
+        w_bf = [sb.tile([P, PASSES, N, PACK], BF16, name="w_bf0", tag="stage", align_bytes=64)]
+        w_codes = [sb.tile([P, PASSES * N], U32, name=f"w_codes{i}", align_bytes=64) for i in range(2)]
+        w_scales = [sb.tile([P, PASSES * N], U8, name=f"w_scales{i}", align_bytes=64) for i in range(2)]
+
+        def quantise(i):
+            nc.vector.quantize_mx(
+                out=w_codes[i][:].bitcast(FP8X4),
+                scales=w_scales[i][:],
+                in_=w_bf[i][:].rearrange("p g n j -> p (g n j)"),
+            )
+
+        picked0 = sb.tile([P, S], U32, name="picked0", align_bytes=64)
+        picked1 = []
+        picked_scales = sb.tile([P, S], U8, name="picked_scales", align_bytes=64)
+
+        def picked_words(o, h):
+            return picked0[:, h * HALF : (h + 1) * HALF] if o == 0 else picked1[h][:]
+
+        def product(acc, i, o, h):
+            nc.tensor.matmul_mx(
+                out=acc[:],
+                lhsT=w_codes[i][:, o * N : (o + 1) * N].bitcast(FP8X4),
+                lhsT_scale=w_scales[i][:, o * N : (o + 1) * N],
+                rhs=picked_words(o, h).bitcast(FP8X4),
+                rhs_scale=picked_scales[4 * o :, h * HALF : (h + 1) * HALF],
+                start=(o == 0),
+                stop=(o == PASSES - 1),
+            )
+
+        def list_half(lst, h):
+            return lst[:, h * HALF // 16 : (h + 1) * HALF // 16]
+
+        nc.vector.tensor_copy(picked0[:], table_words[0][:].indirect(offs_sb[:]))
+        nc.vector.tensor_copy(picked_scales[:], table_scales[:].indirect(offs_sb[:]))
+        nc.scalar.copy(out=w_bf[0][:], in_=w_raw[0][:].rearrange("p g j n -> p g n j"))
+        quantise(0)
+
+        y = [psum.tile([P, HALF], F32, name=f"y{h}") for h in range(2)]
+        z = [psum.tile([P, HALF], F32, name=f"z{h}") for h in range(2)]
+        rho_all = sb.tile([P, S], F32, name="rho_all", align_bytes=64)
+        rho = [rho_all[:, h * HALF : (h + 1) * HALF] for h in range(2)]
+        dens = sb.tile([P, V], F32, name="dens", align_bytes=64)
+        root = sb.tile([P, V], F32, name="root", align_bytes=64)
+        for h in range(2):
+            product(y[h], 0, 0, h)
+        for h in range(2):
+            picked1.append(sb.tile([P, HALF], U32, name=f"picked1_{h}", tag=("stage", "second")[h], align_bytes=64))
+            nc.vector.tensor_copy(picked1[h][:], table_words[1][:].indirect(list_half(offs_sb, h)))
+            product(y[h], 0, 1, h)
+            nc.scalar.activation(out=rho[h], in_=y[h][:], func=ACT.Exp, scale=0.5)
+
+        w_bf.append(sb.tile([P, PASSES, N, PACK], BF16, name="w_bf1", tag="table1", align_bytes=64))
+        nc.vector.tensor_copy(out=w_bf[1][:], in_=w_raw[1][:].rearrange("p g j n -> p g n j"))
+        pairs = rho_all[:].rearrange("p (v d) -> p v d", d=2)
+        nc.vector.scalar_tensor_tensor(
+            out=dens[:], in0=pairs[:, :, 0], scalar=0.5, in1=pairs[:, :, 1], op0=ALU.add, op1=ALU.add
+        )
+        quantise(1)
+        for h in range(2):
+            for o in range(PASSES):
+                product(z[h], 1, o, h)
+
+        near = [sb.tile([P, HALF], F32, name=f"near{h}", align_bytes=64) for h in range(2)]
+        for h in range(2):
+            atoms = slice(h * V // 2, (h + 1) * V // 2)
+            nc.scalar.activation(out=root[:, atoms], in_=dens[:, atoms], func=ACT.Abs_reciprocal_sqrt, scale=4.0)
+        for h in range(2):
+            atoms = slice(h * V // 2, (h + 1) * V // 2)
+            nc.vector.tensor_tensor(out=slope[:, atoms], in0=root[:, atoms], in1=emb_sb[:, atoms], op=ALU.mult)
+            nc.scalar.copy(
+                out=near[h][:].rearrange("p (v d) -> p v d", d=2),
+                in_=slope[:, atoms].unsqueeze(2).to_broadcast([P, V // 2, 2]),
+            )
+
+        both = [sb.tile([P, HALF], F32, name=f"both{h}", align_bytes=64) for h in range(2)]
+        bond = [sb.tile([P, HALF], F32, name=f"bond{h}", align_bytes=64) for h in range(2)]
+        force = [sb.tile([P, HALF], F32, name=f"force{h}", align_bytes=64) for h in range(2)]
+        for h in range(2):
+            nc.vector.tensor_tensor(both[h][:], slope[:].indirect(list_half(nbr_sb, h)), near[h][:], ALU.add)
+        for h in range(2):
+            nc.vector.tensor_tensor(out=bond[h][:], in0=both[h][:], in1=rho[h], op=ALU.mult)
+        for h in range(2):
+            nc.vector.tensor_tensor(out=force[h][:], in0=bond[h][:], in1=z[h][:], op=ALU.add)
+            nc.sync.dma_start(out=out[:, h * HALF : (h + 1) * HALF], in_=force[h][:])

@@ -38,7 +38,8 @@ def tile_picked_yeamf_force_p_kernel(
         emb_sb = sb.tile([P, V], F32, name="emb_sb", align_bytes=64)
         slope = sb.tile([P, V + SPARE], F32, name="slope", align_bytes=64)
 
-        nc.vector.memset(table_scales[:].bitcast(I32), 0)
+        nc.vector.memset(table_scales[:, : T // 2].bitcast(I32), 0)
+        nc.gpsimd.memset(table_scales[:, T // 2 :].bitcast(I32), 0)
         nc.vector.memset(slope[:, V:], 0.0)
 
         def load_words(o):
@@ -53,9 +54,8 @@ def tile_picked_yeamf_force_p_kernel(
                 in_=w.rearrange("(g p j) n -> p g (j n)", p=P, j=PACK),
             )
 
-        nc.sync.dma_start(offs_sb[:], offs)
-        nc.sync.dma_start(nbr_sb[:], nbr)
         load_words(0)
+        nc.sync.dma_start(offs_sb[:], offs)
         load_weight(0, w1)
         for q in range(4):
             nc.sync.dma_start(
@@ -64,6 +64,7 @@ def tile_picked_yeamf_force_p_kernel(
             )
         load_words(1)
         load_weight(1, w2)
+        nc.sync.dma_start(nbr_sb[:], nbr)
         nc.sync.dma_start(out=emb_sb[:], in_=emb)
 
         w_bf = [sb.tile([P, PASSES, N, PACK], BF16, name="w_bf0", tag="stage", align_bytes=64)]
@@ -84,13 +85,13 @@ def tile_picked_yeamf_force_p_kernel(
         def picked_words(o, h):
             return picked0[:, h * HALF : (h + 1) * HALF] if o == 0 else picked1[h][:]
 
-        def product(acc, i, o, h):
+        def product(acc, i, o, h, c0=0, c1=HALF):
             nc.tensor.matmul_mx(
                 out=acc[:],
                 lhsT=w_codes[i][:, o * N : (o + 1) * N].bitcast(FP8X4),
                 lhsT_scale=w_scales[i][:, o * N : (o + 1) * N],
-                rhs=picked_words(o, h).bitcast(FP8X4),
-                rhs_scale=picked_scales[4 * o :, h * HALF : (h + 1) * HALF],
+                rhs=picked_words(o, h)[:, c0:c1].bitcast(FP8X4),
+                rhs_scale=picked_scales[4 * o :, h * HALF + c0 : h * HALF + c1],
                 start=(o == 0),
                 stop=(o == PASSES - 1),
             )
@@ -103,19 +104,21 @@ def tile_picked_yeamf_force_p_kernel(
         nc.scalar.copy(out=w_bf[0][:], in_=w_raw[0][:].rearrange("p g j n -> p g n j"))
         quantise(0)
 
-        y = [psum.tile([P, HALF], F32, name=f"y{h}") for h in range(2)]
+        spans = [(0, 0, HALF), (1, 0, HALF // 2), (1, HALF // 2, HALF)]
+        y = [psum.tile([P, c1 - c0], F32, name=f"y{n}") for n, (h, c0, c1) in enumerate(spans)]
         z = [psum.tile([P, HALF], F32, name=f"z{h}") for h in range(2)]
         rho_all = sb.tile([P, S], F32, name="rho_all", align_bytes=64)
         rho = [rho_all[:, h * HALF : (h + 1) * HALF] for h in range(2)]
         dens = sb.tile([P, V], F32, name="dens", align_bytes=64)
         root = sb.tile([P, V], F32, name="root", align_bytes=64)
-        for h in range(2):
-            product(y[h], 0, 0, h)
+        for n, (h, c0, c1) in enumerate(spans):
+            product(y[n], 0, 0, h, c0, c1)
         for h in range(2):
             picked1.append(sb.tile([P, HALF], U32, name=f"picked1_{h}", tag=("stage", "second")[h], align_bytes=64))
             nc.vector.tensor_copy(picked1[h][:], table_words[1][:].indirect(list_half(offs_sb, h)))
-            product(y[h], 0, 1, h)
-            nc.scalar.activation(out=rho[h], in_=y[h][:], func=ACT.Exp, scale=0.5)
+        for n, (h, c0, c1) in enumerate(spans):
+            product(y[n], 0, 1, h, c0, c1)
+            nc.scalar.activation(out=rho[h][:, c0:c1], in_=y[n][:], func=ACT.Exp, scale=0.5)
 
         w_bf.append(sb.tile([P, PASSES, N, PACK], BF16, name="w_bf1", tag="table1", align_bytes=64))
         nc.vector.tensor_copy(out=w_bf[1][:], in_=w_raw[1][:].rearrange("p g j n -> p g n j"))
@@ -128,25 +131,26 @@ def tile_picked_yeamf_force_p_kernel(
             for o in range(PASSES):
                 product(z[h], 1, o, h)
 
-        near = [sb.tile([P, HALF], F32, name=f"near{h}", align_bytes=64) for h in range(2)]
-        for h in range(2):
-            atoms = slice(h * V // 2, (h + 1) * V // 2)
-            nc.scalar.activation(out=root[:, atoms], in_=dens[:, atoms], func=ACT.Abs_reciprocal_sqrt, scale=4.0)
-        for h in range(2):
-            atoms = slice(h * V // 2, (h + 1) * V // 2)
-            nc.vector.tensor_tensor(out=slope[:, atoms], in0=root[:, atoms], in1=emb_sb[:, atoms], op=ALU.mult)
+        atom_runs = [(0, V // 4), (V // 4, V)]
+        bond_runs = [(0, S // 4), (S // 4, S // 2), (S // 2, S)]
+        for a0, a1 in atom_runs:
+            nc.scalar.activation(out=root[:, a0:a1], in_=dens[:, a0:a1], func=ACT.Abs_reciprocal_sqrt, scale=4.0)
+        for a0, a1 in atom_runs:
+            nc.vector.tensor_tensor(out=slope[:, a0:a1], in0=root[:, a0:a1], in1=emb_sb[:, a0:a1], op=ALU.mult)
+        near = sb.tile([P, S], F32, name="near", align_bytes=64)
+        both = sb.tile([P, S], F32, name="both", align_bytes=64)
+        for j0, j1 in bond_runs:
             nc.scalar.copy(
-                out=near[h][:].rearrange("p (v d) -> p v d", d=2),
-                in_=slope[:, atoms].unsqueeze(2).to_broadcast([P, V // 2, 2]),
+                out=near[:, j0:j1].rearrange("p (v d) -> p v d", d=2),
+                in_=slope[:, j0 // 2 : j1 // 2].unsqueeze(2).to_broadcast([P, (j1 - j0) // 2, 2]),
             )
-
-        both = [sb.tile([P, HALF], F32, name=f"both{h}", align_bytes=64) for h in range(2)]
+            nc.vector.tensor_tensor(
+                both[:, j0:j1], slope[:].indirect(nbr_sb[:, j0 // 16 : j1 // 16]), near[:, j0:j1], ALU.add
+            )
         bond = [sb.tile([P, HALF], F32, name=f"bond{h}", align_bytes=64) for h in range(2)]
         force = [sb.tile([P, HALF], F32, name=f"force{h}", align_bytes=64) for h in range(2)]
         for h in range(2):
-            nc.vector.tensor_tensor(both[h][:], slope[:].indirect(list_half(nbr_sb, h)), near[h][:], ALU.add)
-        for h in range(2):
-            nc.vector.tensor_tensor(out=bond[h][:], in0=both[h][:], in1=rho[h], op=ALU.mult)
+            nc.vector.tensor_tensor(out=bond[h][:], in0=both[:, h * HALF : (h + 1) * HALF], in1=rho[h], op=ALU.mult)
         for h in range(2):
             nc.vector.tensor_tensor(out=force[h][:], in0=bond[h][:], in1=z[h][:], op=ALU.add)
             nc.sync.dma_start(out=out[:, h * HALF : (h + 1) * HALF], in_=force[h][:])

@@ -54,14 +54,27 @@ def tile_picked_yeamf_force_p_kernel(
                 in_=w.rearrange("(g p j) n -> p g (j n)", p=P, j=PACK),
             )
 
-        load_words(0)
-        nc.sync.dma_start(offs_sb[:], offs)
-        load_weight(0, w1)
-        for q in range(4):
+        def load_weight_pass(i, w, o):
             nc.sync.dma_start(
-                out=table_scales[32 * q : 32 * q + 4 * PASSES, :].bitcast(I32),
-                in_=x_scales[:, 4 * q : 4 * q + 4, :].bitcast(I32),
+                out=w_raw[i][:, o, :, :].rearrange("p j n -> p (j n)"),
+                in_=w[o * P * PACK : (o + 1) * P * PACK, :].rearrange("(p j) n -> p (j n)", j=PACK),
             )
+
+        def load_scale_rows(r):
+            for o in range(PASSES):
+                nc.sync.dma_start(
+                    out=table_scales[4 * o + r : P : 32, :].bitcast(I32),
+                    in_=x_scales[o, r:16:4, :].bitcast(I32),
+                )
+
+        load_weight_pass(0, w1, 0)
+        nc.sync.dma_start(offs_sb[:], offs)
+        load_weight_pass(0, w1, 1)
+        load_scale_rows(0)
+        load_scale_rows(1)
+        load_words(0)
+        load_scale_rows(2)
+        load_scale_rows(3)
         load_words(1)
         load_weight(1, w2)
         nc.sync.dma_start(nbr_sb[:], nbr)
@@ -101,7 +114,8 @@ def tile_picked_yeamf_force_p_kernel(
 
         nc.vector.tensor_copy(picked0[:], table_words[0][:].indirect(offs_sb[:]))
         nc.vector.tensor_copy(picked_scales[:], table_scales[:].indirect(offs_sb[:]))
-        nc.scalar.copy(out=w_bf[0][:], in_=w_raw[0][:].rearrange("p g j n -> p g n j"))
+        for o in range(PASSES):
+            nc.scalar.copy(out=w_bf[0][:, o, :, :], in_=w_raw[0][:, o, :, :].rearrange("p j n -> p n j"))
         quantise(0)
 
         spans = [(0, 0, HALF), (1, 0, HALF // 2), (1, HALF // 2, HALF)]

from contextlib import ExitStack

import concourse.mybir as mybir

K, T, S, N, V = 1024, 2048, 512, 128, 256
FLOPS = 2 * 2 * K * N * S

F32 = mybir.dt.float32
BF16 = mybir.dt.bfloat16
I32 = mybir.dt.int32
U32 = mybir.dt.uint32
U16 = mybir.dt.uint16
U8 = mybir.dt.uint8
FP8X4 = mybir.dt.float8_e4m3fn_x4
ACT = mybir.ActivationFunctionType
ALU = mybir.AluOpType

P = 128
PACK = 4
PASSES = K // (P * PACK)
HALF = S // 2
SPARE = 32


def tile_picked_yeamf_force_p_kernel(
    tc, x_words, x_scales, w1, w2, emb, offs, nbr, out
):
    nc = tc.nc
    with ExitStack() as ctx:
        sb = ctx.enter_context(tc.tile_pool(name="sb", bufs=1))
        psum = ctx.enter_context(tc.psum_pool(name="psum", bufs=1))

        offs_sb = sb.tile([P, S // 16], U16, name="offs_sb")
        nbr_sb = sb.tile([P, S // 16], U16, name="nbr_sb")
        table_words = [sb.tile([P, T], U32, name=f"table_words{o}", tag=f"table{o}", align_bytes=64) for o in range(PASSES)]
        table_scales = sb.tile([P, T], U8, name="table_scales", align_bytes=64)
        w_raw = [sb.tile([P, PASSES, PACK, N], F32, name=f"w_raw{i}", align_bytes=64) for i in range(2)]
        emb_sb = sb.tile([P, V], F32, name="emb_sb", align_bytes=64)
        slope = sb.tile([P, V + SPARE], F32, name="slope", align_bytes=64)

        nc.vector.memset(table_scales[:, : T // 2].bitcast(I32), 0)
        nc.gpsimd.memset(table_scales[:, T // 2 :].bitcast(I32), 0)
        nc.vector.memset(slope[:, V:], 0.0)

        def load_words(o):
            nc.sync.dma_start(
                out=table_words[o][:].bitcast(I32),
                in_=x_words[o].rearrange("p c r -> p (c r)").bitcast(I32),
            )

        def load_weight(i, w):
            nc.sync.dma_start(
                out=w_raw[i][:].rearrange("p g j n -> p g (j n)"),
                in_=w.rearrange("(g p j) n -> p g (j n)", p=P, j=PACK),
            )

        def load_weight_pass(i, w, o):
            nc.sync.dma_start(
                out=w_raw[i][:, o, :, :].rearrange("p j n -> p (j n)"),
                in_=w[o * P * PACK : (o + 1) * P * PACK, :].rearrange("(p j) n -> p (j n)", j=PACK),
            )

        def load_scale_rows(r):
            for o in range(PASSES):
                nc.sync.dma_start(
                    out=table_scales[4 * o + r : P : 32, :].bitcast(I32),
                    in_=x_scales[o, r:16:4, :].bitcast(I32),
                )

        load_weight_pass(0, w1, 0)
        nc.sync.dma_start(offs_sb[:], offs)
        load_weight_pass(0, w1, 1)
        load_scale_rows(0)
        load_scale_rows(1)
        load_words(0)
        load_scale_rows(2)
        load_scale_rows(3)
        load_words(1)
        load_weight(1, w2)
        nc.sync.dma_start(nbr_sb[:], nbr)
        nc.sync.dma_start(out=emb_sb[:], in_=emb)

        w_bf = [sb.tile([P, PASSES, N, PACK], BF16, name="w_bf0", tag="stage", align_bytes=64)]
        w_codes = [sb.tile([P, PASSES * N], U32, name=f"w_codes{i}", align_bytes=64) for i in range(2)]
        w_scales = [sb.tile([P, PASSES * N], U8, name=f"w_scales{i}", align_bytes=64) for i in range(2)]

        def quantise(i):
            nc.vector.quantize_mx(
                out=w_codes[i][:].bitcast(FP8X4),
                scales=w_scales[i][:],
                in_=w_bf[i][:].rearrange("p g n j -> p (g n j)"),
            )

        picked0 = sb.tile([P, S], U32, name="picked0", align_bytes=64)
        picked1 = []
        picked_scales = sb.tile([P, S], U8, name="picked_scales", align_bytes=64)

        def picked_words(o, h):
            return picked0[:, h * HALF : (h + 1) * HALF] if o == 0 else picked1[h][:]

        def product(acc, i, o, h, c0=0, c1=HALF):
            nc.tensor.matmul_mx(
                out=acc[:],
                lhsT=w_codes[i][:, o * N : (o + 1) * N].bitcast(FP8X4),
                lhsT_scale=w_scales[i][:, o * N : (o + 1) * N],
                rhs=picked_words(o, h)[:, c0:c1].bitcast(FP8X4),
                rhs_scale=picked_scales[4 * o :, h * HALF + c0 : h * HALF + c1],
                start=(o == 0),
                stop=(o == PASSES - 1),
            )

        def list_half(lst, h):
            return lst[:, h * HALF // 16 : (h + 1) * HALF // 16]

        nc.vector.tensor_copy(picked0[:], table_words[0][:].indirect(offs_sb[:]))
        nc.vector.tensor_copy(picked_scales[:], table_scales[:].indirect(offs_sb[:]))
        for o in range(PASSES):
            nc.scalar.copy(out=w_bf[0][:, o, :, :], in_=w_raw[0][:, o, :, :].rearrange("p j n -> p n j"))
        quantise(0)

        spans = [(0, 0, HALF), (1, 0, HALF // 2), (1, HALF // 2, HALF)]
        y = [psum.tile([P, c1 - c0], F32, name=f"y{n}") for n, (h, c0, c1) in enumerate(spans)]
        z = [psum.tile([P, HALF], F32, name=f"z{h}") for h in range(2)]
        rho_all = sb.tile([P, S], F32, name="rho_all", align_bytes=64)
        rho = [rho_all[:, h * HALF : (h + 1) * HALF] for h in range(2)]
        dens = sb.tile([P, V], F32, name="dens", align_bytes=64)
        root = sb.tile([P, V], F32, name="root", align_bytes=64)
        for n, (h, c0, c1) in enumerate(spans):
            product(y[n], 0, 0, h, c0, c1)
        for h in range(2):
            picked1.append(sb.tile([P, HALF], U32, name=f"picked1_{h}", tag=("stage", "second")[h], align_bytes=64))
            nc.vector.tensor_copy(picked1[h][:], table_words[1][:].indirect(list_half(offs_sb, h)))
        for n, (h, c0, c1) in enumerate(spans):
            product(y[n], 0, 1, h, c0, c1)
            nc.scalar.activation(out=rho[h][:, c0:c1], in_=y[n][:], func=ACT.Exp, scale=0.5)

        w_bf.append(sb.tile([P, PASSES, N, PACK], BF16, name="w_bf1", tag="table1", align_bytes=64))
        nc.vector.tensor_copy(out=w_bf[1][:], in_=w_raw[1][:].rearrange("p g j n -> p g n j"))
        pairs = rho_all[:].rearrange("p (v d) -> p v d", d=2)
        nc.vector.scalar_tensor_tensor(
            out=dens[:], in0=pairs[:, :, 0], scalar=0.5, in1=pairs[:, :, 1], op0=ALU.add, op1=ALU.add
        )
        quantise(1)
        for h in range(2):
            for o in range(PASSES):
                product(z[h], 1, o, h)

        atom_runs = [(0, V // 4), (V // 4, V)]
        bond_runs = [(0, S // 4), (S // 4, S // 2), (S // 2, S)]
        for a0, a1 in atom_runs:
            nc.scalar.activation(out=root[:, a0:a1], in_=dens[:, a0:a1], func=ACT.Abs_reciprocal_sqrt, scale=4.0)
        for a0, a1 in atom_runs:
            nc.vector.tensor_tensor(out=slope[:, a0:a1], in0=root[:, a0:a1], in1=emb_sb[:, a0:a1], op=ALU.mult)
        near = sb.tile([P, S], F32, name="near", align_bytes=64)
        both = sb.tile([P, S], F32, name="both", align_bytes=64)
        for j0, j1 in bond_runs:
            nc.scalar.copy(
                out=near[:, j0:j1].rearrange("p (v d) -> p v d", d=2),
                in_=slope[:, j0 // 2 : j1 // 2].unsqueeze(2).to_broadcast([P, (j1 - j0) // 2, 2]),
            )
            nc.vector.tensor_tensor(
                both[:, j0:j1], slope[:].indirect(nbr_sb[:, j0 // 16 : j1 // 16]), near[:, j0:j1], ALU.add
            )
        bond = [sb.tile([P, HALF], F32, name=f"bond{h}", align_bytes=64) for h in range(2)]
        force = [sb.tile([P, HALF], F32, name=f"force{h}", align_bytes=64) for h in range(2)]
        for h in range(2):
            nc.vector.tensor_tensor(out=bond[h][:], in0=both[:, h * HALF : (h + 1) * HALF], in1=rho[h], op=ALU.mult)
        for h in range(2):
            nc.vector.tensor_tensor(out=force[h][:], in0=bond[h][:], in1=z[h][:], op=ALU.add)
            nc.sync.dma_start(out=out[:, h * HALF : (h + 1) * HALF], in_=force[h][:])
